import numpy as np
import ml_dtypes


def mxq(x, axis, fmt="e4m3"):
    dtype, down = {"e4m3": (ml_dtypes.float8_e4m3fn, 7), "e5m2": (ml_dtypes.float8_e5m2, 14)}[fmt]
    v = np.moveaxis(np.asarray(x, np.float32).astype(ml_dtypes.bfloat16).astype(np.float64), axis, -1)
    blocks = v.reshape(v.shape[:-1] + (-1, 32))
    amax = np.abs(blocks).max(-1, keepdims=True)
    byte = np.maximum(np.where(amax > 0, np.frexp(amax)[1] - 1 + 127, 0) - down, 1)
    scale = np.exp2(byte - 127.0)
    codes = (blocks / scale).astype(np.float32).astype(dtype).astype(np.float64)
    return np.moveaxis((codes * scale).reshape(v.shape), -1, axis)


WIDE = False


def mx_kscale(k):
    if not WIDE:
        return np.ones(k)
    levels = np.array([10, -10, 5, -5, 0])
    if k % 512:
        return np.exp2(np.random.permutation(np.resize(levels, k // 32))).repeat(32)
    a = np.empty((k // 512, 16))
    for p in range(k // 512):
        a[p, :8] = np.random.permutation(np.resize(levels, 8))
        for g in range(8):
            far = levels[np.abs(levels - a[p, g]) >= 10]
            a[p, g + 8] = far[np.random.randint(len(far))]
    return np.exp2(a.ravel()).repeat(32)


def f64(x):
    return np.asarray(x).astype(np.float64)


def striped(idx):
    return np.tile(np.asarray(idx).reshape(-1, 16).T, (8, 1)).astype(np.uint16)


def unstriped(offs):
    return offs[:16].T.reshape(-1).astype(np.int64)


E2M1 = np.array([0.0, 0.5, 1.0, 1.5, 2.0, 3.0, 4.0, 6.0, -0.0, -0.5, -1.0, -1.5, -2.0, -3.0, -4.0, -6.0])


def pack_weight(w, fmt):
    k, n = w.shape
    w = f64(np.asarray(w, np.float32).astype(ml_dtypes.bfloat16)).reshape(k // 32, 32, n)
    amax = np.abs(w).max(1)
    if fmt == "e4m3":
        byte = np.frexp(amax)[1] - 1 + 127 - 7
    else:
        mant, ex = np.frexp(amax / 6.0)
        byte = np.where(mant > 0.5, ex, ex - 1) + 127
    byte = np.clip(np.where(amax > 0, byte, 1), 1, 254)
    scaled = (w * np.exp2(127.0 - byte)[:, None, :]).reshape(k, n).astype(np.float32)
    by_word = np.ascontiguousarray(scaled.reshape(k // 512, 128, 4, n).transpose(0, 1, 3, 2))
    if fmt == "e4m3":
        words = by_word.astype(ml_dtypes.float8_e4m3fn).view(np.uint8)
    else:
        c = by_word.astype(ml_dtypes.float4_e2m1fn).view(np.uint8) & 0xF
        words = (c[..., 0::2] | (c[..., 1::2] << 4)).reshape(k // 512, 128, 2 * n)
    return np.ascontiguousarray(words), np.ascontiguousarray(byte.astype(np.uint8).reshape(k // 512, 16, n))


def unpack_weight(words, scales, fmt):
    g, _, n = scales.shape
    words = np.ascontiguousarray(words).reshape(g, 128, n, -1)
    if fmt == "e4m3":
        vals = words.view(ml_dtypes.float8_e4m3fn).astype(np.float64)
    else:
        nib = np.empty((g, 128, n, 4), np.uint8)
        nib[..., 0::2] = words & 0xF
        nib[..., 1::2] = words >> 4
        vals = E2M1[nib]
    vals = vals * np.repeat(np.exp2(scales.astype(np.float64) - 127.0), 8, axis=1)[..., None]
    return vals.transpose(0, 1, 3, 2).reshape(g * 512, n)


def softplus(v):
    return np.log(1.0 + np.exp(v))


def sigmoid(v):
    return 1.0 / (1.0 + np.exp(-v))


D, E, T, I, Q, U = 512, 512, 1024, 256, 512, 1024


def setup_inputs():
    n = np.random.standard_normal
    idx = np.random.permutation(T)[:I]
    idx4 = np.random.permutation(U)[:I]
    fd = mx_kscale(D)
    fe = mx_kscale(E)
    fq = mx_kscale(Q)
    keysp = pack_weight(n((D, T)) / fd[:, None], "e4m3")
    valsp = pack_weight(n((E, T)) / fe[:, None], "e4m3")
    return {
        "query": (n((D, Q)) * 1.0 / np.sqrt(D) * fd[:, None]).astype(np.float32),
        "keys_words": keysp[0],
        "keys_scales": keysp[1],
        "th": (np.random.uniform(-0.5, 0.5, (Q, 1))).astype(np.float32),
        "reserve": (np.random.uniform(20.0, 100.0, (Q, 1))).astype(np.float32),
        "gout": (n((E, Q)) * 1 / np.sqrt(E) * fe[:, None]).astype(np.float32),
        "vals_words": valsp[0],
        "vals_scales": valsp[1],
        "size": (np.random.uniform(0.5, 2.0, (1, I))).astype(np.float32),
        "qs": (np.random.uniform(100.0, 400.0, (Q, 1)) * fq[:, None]).astype(np.float32),
        "qrows": (n((Q, D)) / fq[:, None]).astype(np.float32),
        "old": (n((D, U)) * 4.0).astype(np.float32),
        "fade": (np.random.uniform(0.5, 1.0, (1, U))).astype(np.float32),
        "offs": striped(idx),
        "offs4": striped(idx4),
    }


def reference(query, keys_words, keys_scales, th, reserve, gout, vals_words, vals_scales, size, qs, qrows, old, fade, offs, offs4):
    idx = unstriped(offs)
    idx4 = unstriped(offs4)
    keysu = unpack_weight(keys_words, keys_scales, "e4m3")
    valsu = unpack_weight(vals_words, vals_scales, "e4m3")
    queryq = mxq(f64(query), 0, "e4m3")
    keysidxg = keysu[:, idx]
    a = queryq.T @ keysidxg
    p = softplus(a - f64(th))
    z = np.sum(p, axis=1, keepdims=True) + f64(reserve)
    goutq = mxq(f64(gout), 0, "e4m3")
    valsidxg = valsu[:, idx]
    c0 = goutq.T @ valsidxg
    dz = np.sum(c0 * p * f64(size) / np.square(z) * (-1.0), axis=1, keepdims=True)
    dp = c0 / z * f64(size) + dz
    da = dp * sigmoid(a - f64(th))
    gs = da * f64(qs)
    qrowsq = mxq(f64(qrows), 0, "e4m3")
    gsq = mxq(gs, 0, "e4m3")
    gk = qrowsq.T @ gsq
    gf = np.zeros((D, U))
    gf[:, idx4] = gk
    y = f64(old) * f64(fade) + gf
    return y

@@ -1,0 +1,240 @@
+from contextlib import ExitStack
+
+import concourse.mybir as mybir
+from concourse.masks import make_identity
+
+D, E, T, I, Q, U = 512, 512, 1024, 256, 512, 1024
+FLOPS = 2 * I * Q * (D + E + D)
+
+F32 = mybir.dt.float32
+BF16 = mybir.dt.bfloat16
+I32 = mybir.dt.int32
+U32 = mybir.dt.uint32
+U16 = mybir.dt.uint16
+U8 = mybir.dt.uint8
+FP8X4 = mybir.dt.float8_e4m3fn_x4
+ALU = mybir.AluOpType
+ACT = mybir.ActivationFunctionType
+
+P = 128
+PACK = 4
+BANK = 512
+QUERY_SPLIT = 80
+
+
+def tile_attend_bsoftthreshold_k_kernel(tc, query, keys_words, keys_scales, th, reserve, gout, vals_words,
+                                         vals_scales, size, qs, qrows, old, fade, offs, offs4, out):
+    nc = tc.nc
+    with ExitStack() as ctx:
+        lists = ctx.enter_context(tc.tile_pool(name="lists", bufs=1))
+        sb = ctx.enter_context(tc.tile_pool(name="sb", bufs=1))
+        ps = ctx.enter_context(tc.psum_pool(name="ps", bufs=1))
+
+        def sbuf(name, shape, dtype):
+            return sb.tile(shape, dtype, name=name, align_bytes=64)
+
+        def bank(tag, shape):
+            return ps.tile(shape, F32, name=tag, tag=tag)
+
+        key_plane = sbuf("key_plane", [P, T], U8)
+        val_plane = sbuf("val_plane", [P, T], U8)
+        half = sbuf("half", [P, 1], F32)
+        nc.vector.memset(half[:], 0.5)
+        minus_half = sbuf("minus_half", [P, 1], F32)
+        nc.vector.memset(minus_half[:], -0.5)
+        warm = sbuf("warm", [P, 1], F32)
+        nc.scalar.activation(warm[:], half[:], ACT.Sigmoid)
+        fade_rows = sbuf("fade_rows", [P, P], F32)
+        size_rows = sbuf("size_rows", [P, P], F32)
+        ident = sbuf("ident", [P, P], F32)
+        make_identity(nc, ident[:])
+
+        slots = lists.tile([P, I // 16], U16, name="slots")
+        places = lists.tile([P, I // 16], U16, name="places")
+        query_raw = sbuf("query_raw", [P, PACK, Q], F32)
+        gout_raw = sbuf("gout_raw", [P, PACK, Q], F32)
+        qrows_raw = sbuf("qrows_raw", [P, PACK, D], F32)
+        key_words = sbuf("key_words", [P, T], U32)
+        val_words = sbuf("val_words", [P, T], U32)
+        th_t = sbuf("th_t", [P, PACK], F32)
+        reserve_t = sbuf("reserve_t", [P, PACK], F32)
+        qs_t = sbuf("qs_t", [P, PACK], F32)
+        old_t = [sbuf("old%d" % g, [P, 2, U], F32) for g in range(2)]
+
+        def load_plane(plane, scales):
+            for quad in range(4):
+                nc.sync.dma_start(plane[32 * quad : 32 * quad + 32, :].bitcast(I32),
+                                  scales[0, 4 * quad : 4 * quad + 4, :].bitcast(I32).partition_broadcast(8))
+
+        def load_words(words, src):
+            nc.sync.dma_start(words[:].bitcast(I32), src[0].rearrange("p n t -> p (n t)").bitcast(I32))
+
+        def by_row(vec):
+            return vec.rearrange("(p r) o -> p (r o)", r=PACK)
+
+        nc.sync.dma_start(query_raw[:], query.rearrange("(p j) q -> p j q", j=PACK))
+        nc.sync.dma_start(slots[:], offs)
+        load_words(key_words, keys_words)
+        load_plane(key_plane, keys_scales)
+        nc.sync.dma_start(gout_raw[:], gout.rearrange("(p j) q -> p j q", j=PACK))
+        nc.sync.dma_start(th_t[:], by_row(th))
+        load_words(val_words, vals_words)
+        load_plane(val_plane, vals_scales)
+        nc.sync.dma_start(size_rows[:], size.rearrange("o (c x) -> (o c) x", x=P).partition_broadcast(64))
+        nc.sync.dma_start(qrows_raw[:], qrows.rearrange("(p j) d -> p j d", j=PACK))
+        nc.sync.dma_start(reserve_t[:], by_row(reserve))
+        nc.sync.dma_start(qs_t[:], by_row(qs))
+        nc.sync.dma_start(fade_rows[:], fade.rearrange("o (b x) -> (o b) x", x=P).partition_broadcast(16))
+        for g in range(2):
+            nc.sync.dma_start(old_t[g][:], old[2 * P * g : 2 * P * (g + 1), :].rearrange("(j p) u -> p j u", p=P))
+        nc.sync.dma_start(places[:], offs4)
+
+        windows = [sbuf("window%d" % j, [P, U], F32) for j in range(4)]
+        for j in range(4):
+            nc.vector.memset(windows[j][:], 0.0)
+
+        def deal(engine_copy, dealt, raw, s0, s1):
+            engine_copy(dealt[:, :, s0:s1, :].rearrange("p r s j -> p s j r"),
+                        raw[:].rearrange("p j (s r) -> p s j r", r=PACK)[:, s0:s1])
+
+        def quantize(name, src, width):
+            codes = sbuf(name + "_codes", [P, width], U32)
+            plane = sbuf(name + "_scales", [P, width], U8)
+            nc.vector.quantize_mx(out=codes[:].bitcast(FP8X4), scales=plane[:], in_=src)
+            return codes, plane
+
+        def gather(name, words, plane):
+            g_words = sbuf(name + "_g_words", [P, I], U32)
+            g_plane = sbuf(name + "_g_plane", [P, I], U8)
+            nc.vector.tensor_copy(g_words[:], words[:].indirect(slots[:]))
+            nc.vector.tensor_copy(g_plane[:], plane[:].indirect(slots[:]))
+            return g_words, g_plane
+
+        def product(tags, stationary, moving):
+            banks = [bank(tag, [P, 2, I]) for tag in tags]
+            for m in range(4):
+                cols = slice(m * P, (m + 1) * P)
+                nc.tensor.matmul_mx(out=banks[m // 2][:, m % 2, :],
+                                    lhsT=stationary[0][:, cols].bitcast(FP8X4), lhsT_scale=stationary[1][:, cols],
+                                    rhs=moving[0][:].bitcast(FP8X4), rhs_scale=moving[1][:],
+                                    start=True, stop=True)
+            return banks
+
+        query_dealt = sbuf("query_dealt", [P, PACK, P, PACK], BF16)
+        deal(nc.vector.tensor_copy, query_dealt, query_raw, 0, QUERY_SPLIT)
+        deal(nc.scalar.copy, query_dealt, query_raw, QUERY_SPLIT, P)
+        keys_g = gather("keys", key_words, key_plane)
+        query_q = quantize("query", query_dealt[:].rearrange("p r s j -> p (r s j)"), Q)
+        a_banks = product(["A0", "A1"], query_q, keys_g)
+
+        neg_th = sbuf("neg_th", [P, PACK], F32)
+        nc.vector.tensor_scalar(neg_th[:], th_t[:], -1.0, None, ALU.mult)
+        base = sbuf("base", [P, PACK], F32)
+        nc.vector.scalar_tensor_tensor(base[:], th_t[:], -float(I), reserve_t[:], ALU.mult, ALU.add)
+
+        turned = bank("X0", [P, P])
+        nc.tensor.transpose(turned[:], size_rows[:], ident[:])
+        size_cols = sbuf("size_cols", [P, 2], F32)
+        nc.scalar.copy(size_cols[:], turned[:, 0:2])
+        turned_fade = bank("Y0", [P, P])
+        nc.tensor.transpose(turned_fade[:], fade_rows[:], ident[:])
+        cols_t = sbuf("cols_t", [P, 8], F32)
+        nc.scalar.copy(cols_t[:], turned_fade[:, 0:8])
+        spread = bank("X1", [P, 2, P])
+        for c in range(2):
+            nc.tensor.transpose(spread[:, c, :], size_cols[:, c : c + 1].to_broadcast([P, P]), ident[:])
+        size_t = sbuf("size_t", [P, I], F32)
+        nc.scalar.copy(size_t[:], spread[:].rearrange("p c x -> p (c x)"))
+
+        sig = sbuf("sig", [P, PACK, I], F32)
+        for r in range(PACK):
+            nc.scalar.activation(sig[:, r, :], a_banks[r // 2][:, r % 2, :], ACT.Sigmoid, bias=neg_th[:, r : r + 1])
+        dist = sbuf("dist", [P, PACK * I], F32)
+        nc.scalar.activation(dist[:], sig[:].rearrange("p r i -> p (r i)"), ACT.Abs, bias=minus_half[:])
+        logm = sbuf("logm", [P, PACK, I], F32)
+        for r in range(PACK):
+            nc.scalar.activation(logm[:, r, :], dist[:, r * I : (r + 1) * I], ACT.Ln, bias=half[:])
+
+        gout_dealt = sbuf("gout_dealt", [P, PACK, P, PACK], BF16)
+        deal(nc.vector.tensor_copy, gout_dealt, gout_raw, 0, P)
+        vals_g = gather("vals", val_words, val_plane)
+        gout_q = quantize("gout", gout_dealt[:].rearrange("p r s j -> p (r s j)"), Q)
+        c_banks = product(["C0", "C1"], gout_q, vals_g)
+        cs = sbuf("cs", [P, PACK, I], F32)
+        for h in range(2):
+            nc.vector.tensor_tensor(cs[:, 2 * h : 2 * h + 2, :], c_banks[h][:],
+                                    size_t[:].unsqueeze(1).to_broadcast([P, 2, I]), ALU.mult)
+
+        part = sbuf("part", [P, PACK, I], F32)
+        sum_part = sbuf("sum_part", [P, PACK], F32)
+        for r in range(PACK):
+            nc.vector.scalar_tensor_tensor(part[:, r, :], a_banks[r // 2][:, r % 2, :], th_t[:, r : r + 1],
+                                           logm[:, r, :], ALU.max, ALU.subtract, accum_out=sum_part[:, r : r + 1])
+        weighted = sbuf("weighted", [P, PACK, I], F32)
+        sum_cp = sbuf("sum_cp", [P, PACK], F32)
+
+        def weigh(r):
+            nc.vector.scalar_tensor_tensor(weighted[:, r, :], part[:, r, :], th_t[:, r : r + 1], cs[:, r, :],
+                                           ALU.subtract, ALU.mult, accum_out=sum_cp[:, r : r + 1])
+
+        z = sbuf("z", [P, PACK], F32)
+        inv_z = sbuf("inv_z", [P, PACK], F32)
+        slope = sbuf("slope", [P, PACK], F32)
+        neg = sbuf("neg", [P, PACK], F32)
+        shift = sbuf("shift", [P, PACK], F32)
+        weigh(0)
+        nc.vector.tensor_tensor(z[:], sum_part[:], base[:], ALU.add)
+        weigh(1)
+        nc.vector.reciprocal(inv_z[:], z[:])
+        weigh(2)
+        nc.vector.tensor_tensor(slope[:], qs_t[:], inv_z[:], ALU.mult)
+        weigh(3)
+        nc.vector.scalar_tensor_tensor(neg[:], inv_z[:], -1.0, slope[:], ALU.mult, ALU.mult)
+        nc.vector.tensor_tensor(shift[:], sum_cp[:], neg[:], ALU.mult)
+
+        qrows_il = sbuf("qrows_il", [P, D, PACK], BF16)
+        nc.scalar.copy(qrows_il[:].rearrange("p (c i) t -> p c t i", i=4),
+                       qrows_raw[:].rearrange("p t (c i) -> p c t i", i=4))
+
+        dp = sbuf("dp", [P, PACK, I], F32)
+        for r in range(PACK):
+            nc.vector.tensor_scalar(dp[:, r, :], cs[:, r, :], slope[:, r : r + 1], shift[:, r : r + 1],
+                                    ALU.mult, ALU.add)
+        qrows_q = quantize("qrows", qrows_il[:].rearrange("p d t -> p (d t)"), D)
+        gs = sbuf("gs", [P, I, PACK], BF16)
+        nc.vector.tensor_tensor(gs[:].rearrange("p (c i) r -> p c r i", i=4),
+                                dp[:].rearrange("p r (c i) -> p c r i", i=4),
+                                sig[:].rearrange("p r (c i) -> p c r i", i=4), ALU.mult)
+        gs_q = quantize("gs", gs[:].rearrange("p i r -> p (i r)"), I)
+        g_banks = product(["C0", "C1"], qrows_q, gs_q)
+        gk = [sbuf("gk%d" % j, [P, I], F32) for j in range(4)]
+        for j in range(4):
+            nc.scalar.copy(gk[j][:], g_banks[j // 2][:, j % 2, :])
+
+        faded_tags = [("Y0", "Y1"), ("A0", "A1"), ("X0", "X1"), ("C0", "C1")]
+        faded_t = []
+        for g in range(2):
+            ft = sbuf("faded_t%d" % g, [P, 8, 2, P], F32)
+            faded_t.append(ft)
+            for bb in range(4):
+                stage = bank("X%d" % (bb % 2), [P, 2, 2, P])
+                for b2 in range(2):
+                    b = 2 * bb + b2
+                    for jj in range(2):
+                        nc.tensor.transpose(stage[:, b2, jj, :], old_t[g][:, jj, b * P : (b + 1) * P], ident[:])
+                for b2 in range(2):
+                    b = 2 * bb + b2
+                    nc.scalar.activation(ft[:, b].rearrange("p j d -> p (j d)"),
+                                         stage[:, b2].rearrange("p j d -> p (j d)"), ACT.Copy,
+                                         scale=cols_t[:, b : b + 1])
+
+        for j in range(4):
+            faded = [bank(tag, [P, 4, P]) for tag in faded_tags[j]]
+            for b in range(8):
+                nc.tensor.transpose(faded[b // 4][:, b % 4, :], faded_t[j // 2][:, b, j % 2, :], ident[:])
+            nc.vector.tensor_copy(windows[j][:].indirect(places[:]), gk[j][:])
+            for h in range(2):
+                res = sbuf("res%d_%d" % (j, h), [P, BANK], F32)
+                nc.vector.tensor_tensor(res[:], faded[h][:].rearrange("p b d -> p (b d)"),
+                                        windows[j][:, h * BANK : (h + 1) * BANK], ALU.add)
+                nc.sync.dma_start(out[j * P : (j + 1) * P, h * BANK : (h + 1) * BANK], res[:])

@@ -19,7 +19,6 @@ ACT = mybir.ActivationFunctionType
 P = 128
 PACK = 4
 BANK = 512
-QUERY_SPLIT = 80
 
 
 def tile_attend_bsoftthreshold_k_kernel(tc, query, keys_words, keys_scales, th, reserve, gout, vals_words,
@@ -30,8 +29,8 @@ def tile_attend_bsoftthreshold_k_kernel(tc, query, keys_words, keys_scales, th, 
         sb = ctx.enter_context(tc.tile_pool(name="sb", bufs=1))
         ps = ctx.enter_context(tc.psum_pool(name="ps", bufs=1))
 
-        def sbuf(name, shape, dtype):
-            return sb.tile(shape, dtype, name=name, align_bytes=64)
+        def sbuf(name, shape, dtype, tag=None):
+            return sb.tile(shape, dtype, name=name, tag=tag or name, align_bytes=64)
 
         def bank(tag, shape):
             return ps.tile(shape, F32, name=tag, tag=tag)
@@ -42,17 +41,18 @@ def tile_attend_bsoftthreshold_k_kernel(tc, query, keys_words, keys_scales, th, 
         nc.vector.memset(half[:], 0.5)
         minus_half = sbuf("minus_half", [P, 1], F32)
         nc.vector.memset(minus_half[:], -0.5)
-        warm = sbuf("warm", [P, 1], F32)
-        nc.scalar.activation(warm[:], half[:], ACT.Sigmoid)
         fade_rows = sbuf("fade_rows", [P, P], F32)
-        size_rows = sbuf("size_rows", [P, P], F32)
+        size_t = sbuf("size_t", [P, I], F32)
+        windows = [sbuf("window%d" % j, [P, U], F32) for j in range(4)]
+        for j in range(4):
+            (nc.vector if j < 2 else nc.gpsimd).memset(windows[j][:], 0.0)
         ident = sbuf("ident", [P, P], F32)
         make_identity(nc, ident[:])
 
         slots = lists.tile([P, I // 16], U16, name="slots")
         places = lists.tile([P, I // 16], U16, name="places")
-        query_raw = sbuf("query_raw", [P, PACK, Q], F32)
-        gout_raw = sbuf("gout_raw", [P, PACK, Q], F32)
+        query_raw = [sbuf("query_raw%d" % h, [P, PACK, Q // 2], F32) for h in range(2)]
+        gout_raw = [sbuf("gout_raw%d" % h, [P, PACK, Q // 2], F32) for h in range(2)]
         qrows_raw = sbuf("qrows_raw", [P, PACK, D], F32)
         key_words = sbuf("key_words", [P, T], U32)
         val_words = sbuf("val_words", [P, T], U32)
@@ -61,10 +61,10 @@ def tile_attend_bsoftthreshold_k_kernel(tc, query, keys_words, keys_scales, th, 
         qs_t = sbuf("qs_t", [P, PACK], F32)
         old_t = [sbuf("old%d" % g, [P, 2, U], F32) for g in range(2)]
 
-        def load_plane(plane, scales):
-            for quad in range(4):
-                nc.sync.dma_start(plane[32 * quad : 32 * quad + 32, :].bitcast(I32),
-                                  scales[0, 4 * quad : 4 * quad + 4, :].bitcast(I32).partition_broadcast(8))
+        def load_plane(queue, plane, scales, quads):
+            for quad in quads:
+                queue.dma_start(plane[32 * quad : 32 * quad + 32, :].bitcast(I32),
+                                scales[0, 4 * quad : 4 * quad + 4, :].bitcast(I32).partition_broadcast(8))
 
         def load_words(words, src):
             nc.sync.dma_start(words[:].bitcast(I32), src[0].rearrange("p n t -> p (n t)").bitcast(I32))
@@ -72,30 +72,35 @@ def tile_attend_bsoftthreshold_k_kernel(tc, query, keys_words, keys_scales, th, 
         def by_row(vec):
             return vec.rearrange("(p r) o -> p (r o)", r=PACK)
 
-        nc.sync.dma_start(query_raw[:], query.rearrange("(p j) q -> p j q", j=PACK))
+        def load_half(raw, src, h):
+            cols = slice(h * (Q // 2), (h + 1) * (Q // 2))
+            nc.sync.dma_start(raw[h][:], src[:, cols].rearrange("(p j) q -> p j q", j=PACK))
+
+        load_half(query_raw, query, 0)
         nc.sync.dma_start(slots[:], offs)
+        load_plane(nc.sync, key_plane, keys_scales, range(4))
+        load_half(query_raw, query, 1)
         load_words(key_words, keys_words)
-        load_plane(key_plane, keys_scales)
-        nc.sync.dma_start(gout_raw[:], gout.rearrange("(p j) q -> p j q", j=PACK))
         nc.sync.dma_start(th_t[:], by_row(th))
+        load_plane(nc.sync, val_plane, vals_scales, range(4))
+        load_half(gout_raw, gout, 0)
+        load_half(gout_raw, gout, 1)
         load_words(val_words, vals_words)
-        load_plane(val_plane, vals_scales)
-        nc.sync.dma_start(size_rows[:], size.rearrange("o (c x) -> (o c) x", x=P).partition_broadcast(64))
+        nc.sync.dma_start(fade_rows[:], fade.rearrange("o (b x) -> (o b) x", x=P).partition_broadcast(16))
+        nc.sync.dma_start(size_t[:], size[0].partition_broadcast(P))
         nc.sync.dma_start(qrows_raw[:], qrows.rearrange("(p j) d -> p j d", j=PACK))
         nc.sync.dma_start(reserve_t[:], by_row(reserve))
         nc.sync.dma_start(qs_t[:], by_row(qs))
-        nc.sync.dma_start(fade_rows[:], fade.rearrange("o (b x) -> (o b) x", x=P).partition_broadcast(16))
         for g in range(2):
             nc.sync.dma_start(old_t[g][:], old[2 * P * g : 2 * P * (g + 1), :].rearrange("(j p) u -> p j u", p=P))
         nc.sync.dma_start(places[:], offs4)
 
-        windows = [sbuf("window%d" % j, [P, U], F32) for j in range(4)]
-        for j in range(4):
-            nc.vector.memset(windows[j][:], 0.0)
+        warm = sbuf("warm", [P, 1], F32)
+        nc.scalar.activation(warm[:], half[:], ACT.Sigmoid)
 
-        def deal(engine_copy, dealt, raw, s0, s1):
-            engine_copy(dealt[:, :, s0:s1, :].rearrange("p r s j -> p s j r"),
-                        raw[:].rearrange("p j (s r) -> p s j r", r=PACK)[:, s0:s1])
+        def deal(engine_copy, dealt, raw, h, s0, s1):
+            engine_copy(dealt[:, :, 64 * h + s0 : 64 * h + s1, :].rearrange("p r s j -> p s j r"),
+                        raw[h][:].rearrange("p j (s r) -> p s j r", r=PACK)[:, s0:s1])
 
         def quantize(name, src, width):
             codes = sbuf(name + "_codes", [P, width], U32)
@@ -103,72 +108,59 @@ def tile_attend_bsoftthreshold_k_kernel(tc, query, keys_words, keys_scales, th, 
             nc.vector.quantize_mx(out=codes[:].bitcast(FP8X4), scales=plane[:], in_=src)
             return codes, plane
 
-        def gather(name, words, plane):
-            g_words = sbuf(name + "_g_words", [P, I], U32)
-            g_plane = sbuf(name + "_g_plane", [P, I], U8)
-            nc.vector.tensor_copy(g_words[:], words[:].indirect(slots[:]))
-            nc.vector.tensor_copy(g_plane[:], plane[:].indirect(slots[:]))
-            return g_words, g_plane
+        def gather(name, window, dtype):
+            picked = sbuf(name, [P, I], dtype)
+            nc.vector.tensor_copy(picked[:], window[:].indirect(slots[:]))
+            return picked
 
-        def product(tags, stationary, moving):
-            banks = [bank(tag, [P, 2, I]) for tag in tags]
-            for m in range(4):
-                cols = slice(m * P, (m + 1) * P)
-                nc.tensor.matmul_mx(out=banks[m // 2][:, m % 2, :],
-                                    lhsT=stationary[0][:, cols].bitcast(FP8X4), lhsT_scale=stationary[1][:, cols],
-                                    rhs=moving[0][:].bitcast(FP8X4), rhs_scale=moving[1][:],
-                                    start=True, stop=True)
-            return banks
+        def product(m, dst, stationary, moving):
+            cols = slice(m * P, (m + 1) * P)
+            nc.tensor.matmul_mx(out=dst, lhsT=stationary[0][:, cols].bitcast(FP8X4), lhsT_scale=stationary[1][:, cols],
+                                rhs=moving[0][:].bitcast(FP8X4), rhs_scale=moving[1][:], start=True, stop=True)
 
+        key_plane_g = gather("key_plane_g", key_plane, U8)
         query_dealt = sbuf("query_dealt", [P, PACK, P, PACK], BF16)
-        deal(nc.vector.tensor_copy, query_dealt, query_raw, 0, QUERY_SPLIT)
-        deal(nc.scalar.copy, query_dealt, query_raw, QUERY_SPLIT, P)
-        keys_g = gather("keys", key_words, key_plane)
+        deal(nc.scalar.copy, query_dealt, query_raw, 0, 0, 64)
+        deal(nc.scalar.copy, query_dealt, query_raw, 1, 0, 20)
+        deal(nc.vector.tensor_copy, query_dealt, query_raw, 1, 20, 64)
         query_q = quantize("query", query_dealt[:].rearrange("p r s j -> p (r s j)"), Q)
-        a_banks = product(["A0", "A1"], query_q, keys_g)
+        key_words_g = gather("key_words_g", key_words, U32)
+        scores = [bank(tag, [P, I]) for tag in ("A0", "A1", "Y0", "Y1")]
+        for r in range(PACK):
+            product(r, scores[r][:], query_q, (key_words_g, key_plane_g))
 
         neg_th = sbuf("neg_th", [P, PACK], F32)
-        nc.vector.tensor_scalar(neg_th[:], th_t[:], -1.0, None, ALU.mult)
+        nc.gpsimd.tensor_scalar(neg_th[:], th_t[:], -1.0, 0.0, ALU.mult, ALU.add)
+        th_sum = sbuf("th_sum", [P, PACK], F32)
+        nc.gpsimd.tensor_scalar(th_sum[:], th_t[:], -float(I), 0.0, ALU.mult, ALU.add)
         base = sbuf("base", [P, PACK], F32)
-        nc.vector.scalar_tensor_tensor(base[:], th_t[:], -float(I), reserve_t[:], ALU.mult, ALU.add)
-
-        turned = bank("X0", [P, P])
-        nc.tensor.transpose(turned[:], size_rows[:], ident[:])
-        size_cols = sbuf("size_cols", [P, 2], F32)
-        nc.scalar.copy(size_cols[:], turned[:, 0:2])
-        turned_fade = bank("Y0", [P, P])
-        nc.tensor.transpose(turned_fade[:], fade_rows[:], ident[:])
-        cols_t = sbuf("cols_t", [P, 8], F32)
-        nc.scalar.copy(cols_t[:], turned_fade[:, 0:8])
-        spread = bank("X1", [P, 2, P])
-        for c in range(2):
-            nc.tensor.transpose(spread[:, c, :], size_cols[:, c : c + 1].to_broadcast([P, P]), ident[:])
-        size_t = sbuf("size_t", [P, I], F32)
-        nc.scalar.copy(size_t[:], spread[:].rearrange("p c x -> p (c x)"))
+        nc.gpsimd.tensor_tensor(base[:], th_sum[:], reserve_t[:], ALU.add)
 
         sig = sbuf("sig", [P, PACK, I], F32)
         for r in range(PACK):
-            nc.scalar.activation(sig[:, r, :], a_banks[r // 2][:, r % 2, :], ACT.Sigmoid, bias=neg_th[:, r : r + 1])
+            nc.scalar.activation(sig[:, r, :], scores[r][:], ACT.Sigmoid, bias=neg_th[:, r : r + 1])
         dist = sbuf("dist", [P, PACK * I], F32)
         nc.scalar.activation(dist[:], sig[:].rearrange("p r i -> p (r i)"), ACT.Abs, bias=minus_half[:])
         logm = sbuf("logm", [P, PACK, I], F32)
         for r in range(PACK):
             nc.scalar.activation(logm[:, r, :], dist[:, r * I : (r + 1) * I], ACT.Ln, bias=half[:])
 
+        val_plane_g = gather("val_plane_g", val_plane, U8)
         gout_dealt = sbuf("gout_dealt", [P, PACK, P, PACK], BF16)
-        deal(nc.vector.tensor_copy, gout_dealt, gout_raw, 0, P)
-        vals_g = gather("vals", val_words, val_plane)
+        deal(nc.vector.tensor_copy, gout_dealt, gout_raw, 0, 0, 64)
+        deal(nc.vector.tensor_copy, gout_dealt, gout_raw, 1, 0, 64)
         gout_q = quantize("gout", gout_dealt[:].rearrange("p r s j -> p (r s j)"), Q)
-        c_banks = product(["C0", "C1"], gout_q, vals_g)
+        val_words_g = gather("val_words_g", val_words, U32)
         cs = sbuf("cs", [P, PACK, I], F32)
-        for h in range(2):
-            nc.vector.tensor_tensor(cs[:, 2 * h : 2 * h + 2, :], c_banks[h][:],
-                                    size_t[:].unsqueeze(1).to_broadcast([P, 2, I]), ALU.mult)
+        for r, tag in enumerate(("C0", "C1", "X0", "X1")):
+            c0 = bank(tag, [P, I])
+            product(r, c0[:], gout_q, (val_words_g, val_plane_g))
+            nc.vector.tensor_tensor(cs[:, r, :], c0[:], size_t[:], ALU.mult)
 
         part = sbuf("part", [P, PACK, I], F32)
         sum_part = sbuf("sum_part", [P, PACK], F32)
         for r in range(PACK):
-            nc.vector.scalar_tensor_tensor(part[:, r, :], a_banks[r // 2][:, r % 2, :], th_t[:, r : r + 1],
+            nc.vector.scalar_tensor_tensor(part[:, r, :], scores[r][:], th_t[:, r : r + 1],
                                            logm[:, r, :], ALU.max, ALU.subtract, accum_out=sum_part[:, r : r + 1])
         weighted = sbuf("weighted", [P, PACK, I], F32)
         sum_cp = sbuf("sum_cp", [P, PACK], F32)
@@ -192,9 +184,16 @@ def tile_attend_bsoftthreshold_k_kernel(tc, query, keys_words, keys_scales, th, 
         nc.vector.scalar_tensor_tensor(neg[:], inv_z[:], -1.0, slope[:], ALU.mult, ALU.mult)
         nc.vector.tensor_tensor(shift[:], sum_cp[:], neg[:], ALU.mult)
 
+        turned_fade = bank("X0", [P, P])
+        nc.tensor.transpose(turned_fade[:], fade_rows[:], ident[:])
+        cols_t = sbuf("cols_t", [P, 8], F32)
+        nc.scalar.copy(cols_t[:], turned_fade[:, 0:8])
+
         qrows_il = sbuf("qrows_il", [P, D, PACK], BF16)
-        nc.scalar.copy(qrows_il[:].rearrange("p (c i) t -> p c t i", i=4),
-                       qrows_raw[:].rearrange("p t (c i) -> p c t i", i=4))
+        nc.gpsimd.tensor_scalar(qrows_il[:, 0 : D // 2, :], qrows_raw[:, :, 0 : D // 2].rearrange("p t d -> p d t"),
+                                1.0, 0.0, ALU.mult, ALU.add)
+        nc.scalar.copy(qrows_il[:, D // 2 :, :].rearrange("p (c i) t -> p c t i", i=4),
+                       qrows_raw[:, :, D // 2 :].rearrange("p t (c i) -> p c t i", i=4))
 
         dp = sbuf("dp", [P, PACK, I], F32)
         for r in range(PACK):
@@ -206,18 +205,11 @@ def tile_attend_bsoftthreshold_k_kernel(tc, query, keys_words, keys_scales, th, 
                                 dp[:].rearrange("p r (c i) -> p c r i", i=4),
                                 sig[:].rearrange("p r (c i) -> p c r i", i=4), ALU.mult)
         gs_q = quantize("gs", gs[:].rearrange("p i r -> p (i r)"), I)
-        g_banks = product(["C0", "C1"], qrows_q, gs_q)
-        gk = [sbuf("gk%d" % j, [P, I], F32) for j in range(4)]
-        for j in range(4):
-            nc.scalar.copy(gk[j][:], g_banks[j // 2][:, j % 2, :])
 
-        faded_tags = [("Y0", "Y1"), ("A0", "A1"), ("X0", "X1"), ("C0", "C1")]
-        faded_t = []
-        for g in range(2):
+        def fade_pair(g, tags):
             ft = sbuf("faded_t%d" % g, [P, 8, 2, P], F32)
-            faded_t.append(ft)
             for bb in range(4):
-                stage = bank("X%d" % (bb % 2), [P, 2, 2, P])
+                stage = bank(tags[bb], [P, 2, 2, P])
                 for b2 in range(2):
                     b = 2 * bb + b2
                     for jj in range(2):
@@ -227,14 +219,56 @@ def tile_attend_bsoftthreshold_k_kernel(tc, query, keys_words, keys_scales, th, 
                     nc.scalar.activation(ft[:, b].rearrange("p j d -> p (j d)"),
                                          stage[:, b2].rearrange("p j d -> p (j d)"), ACT.Copy,
                                          scale=cols_t[:, b : b + 1])
+            return ft
 
-        for j in range(4):
-            faded = [bank(tag, [P, 4, P]) for tag in faded_tags[j]]
-            for b in range(8):
-                nc.tensor.transpose(faded[b // 4][:, b % 4, :], faded_t[j // 2][:, b, j % 2, :], ident[:])
+        def turn_back(ft, j, h, tag):
+            faded = bank(tag, [P, 4, P])
+            for b in range(4):
+                nc.tensor.transpose(faded[:, b, :], ft[:, 4 * h + b, j % 2, :], ident[:])
+            return faded[:].rearrange("p b d -> p (b d)")
+
+        def to_sbuf(j, h, faded):
+            held = sbuf("held%d_%d" % (j, h), [P, BANK], F32)
+            nc.scalar.copy(held[:], faded)
+            return held[:]
+
+        def scatter(j):
             nc.vector.tensor_copy(windows[j][:].indirect(places[:]), gk[j][:])
+
+        def finish(engine, queue, j, h, faded):
+            res = sbuf("res%d_%d" % (j, h), [P, BANK], F32)
+            engine.tensor_tensor(res[:], faded, windows[j][:, h * BANK : (h + 1) * BANK], ALU.add)
+            queue.dma_start(out[j * P : (j + 1) * P, h * BANK : (h + 1) * BANK], res[:])
+
+        ft0 = fade_pair(0, ("X0", "X1", "C0", "C1"))
+        gk = [sbuf("gk%d" % j, [P, I], F32) for j in range(4)]
+        first = bank("C1", [P, I])
+        product(0, first[:], qrows_q, gs_q)
+        nc.vector.tensor_copy(gk[0][:], first[:])
+        faded = {}
+        for j in range(2):
             for h in range(2):
-                res = sbuf("res%d_%d" % (j, h), [P, BANK], F32)
-                nc.vector.tensor_tensor(res[:], faded[h][:].rearrange("p b d -> p (b d)"),
-                                        windows[j][:, h * BANK : (h + 1) * BANK], ALU.add)
-                nc.sync.dma_start(out[j * P : (j + 1) * P, h * BANK : (h + 1) * BANK], res[:])
+                faded[j, h] = to_sbuf(j, h, turn_back(ft0, j, h, "AY"[j] + str(h)))
+        middle = bank("C0", [P, 2, I])
+        for j in (1, 2):
+            product(j, middle[:, j - 1, :], qrows_q, gs_q)
+        for j in (1, 2):
+            nc.scalar.copy(gk[j][:], middle[:, j - 1, :])
+        last = bank("C1", [P, I])
+        product(3, last[:], qrows_q, gs_q)
+        nc.scalar.copy(gk[3][:], last[:])
+
+        ft1 = fade_pair(1, ("X0", "X1", "X0", "X1"))
+        faded[2, 0] = to_sbuf(2, 0, turn_back(ft1, 2, 0, "A0"))
+        faded[2, 1] = turn_back(ft1, 2, 1, "A1")
+        for h in range(2):
+            faded[3, h] = turn_back(ft1, 3, h, "Y%d" % h)
+
+        for j in range(3):
+            scatter(j)
+        for j, h in ((0, 0), (0, 1), (1, 0), (1, 1), (2, 0)):
+            finish(nc.gpsimd, nc.sync, j, h, faded[j, h])
+        finish(nc.vector, nc.scalar, 2, 1, faded[2, 1])
+        scatter(3)
+        for h in range(2):
+            finish(nc.vector, nc.scalar, 3, h, faded[3, h])

@@ -88,9 +88,9 @@ def tile_attend_bsoftthreshold_k_kernel(tc, query, keys_words, keys_scales, th, 
         load_words(val_words, vals_words)
         nc.sync.dma_start(fade_rows[:], fade.rearrange("o (b x) -> (o b) x", x=P).partition_broadcast(16))
         nc.sync.dma_start(size_t[:], size[0].partition_broadcast(P))
-        nc.sync.dma_start(qrows_raw[:], qrows.rearrange("(p j) d -> p j d", j=PACK))
         nc.sync.dma_start(reserve_t[:], by_row(reserve))
         nc.sync.dma_start(qs_t[:], by_row(qs))
+        nc.sync.dma_start(qrows_raw[:], qrows.rearrange("(p j) d -> p j d", j=PACK))
         for g in range(2):
             nc.sync.dma_start(old_t[g][:], old[2 * P * g : 2 * P * (g + 1), :].rearrange("(j p) u -> p j u", p=P))
         nc.sync.dma_start(places[:], offs4)
@@ -151,6 +151,11 @@ def tile_attend_bsoftthreshold_k_kernel(tc, query, keys_words, keys_scales, th, 
         deal(nc.vector.tensor_copy, gout_dealt, gout_raw, 1, 0, 64)
         gout_q = quantize("gout", gout_dealt[:].rearrange("p r s j -> p (r s j)"), Q)
         val_words_g = gather("val_words_g", val_words, U32)
+        turned_fade = bank("X0", [P, P])
+        nc.tensor.transpose(turned_fade[:], fade_rows[:], ident[:])
+        cols_t = sbuf("cols_t", [P, 8], F32)
+        nc.vector.tensor_copy(cols_t[:], turned_fade[:, 0:8])
+
         cs = sbuf("cs", [P, PACK, I], F32)
         for r, tag in enumerate(("C0", "C1", "X0", "X1")):
             c0 = bank(tag, [P, I])
@@ -174,40 +179,49 @@ def tile_attend_bsoftthreshold_k_kernel(tc, query, keys_words, keys_scales, th, 
         slope = sbuf("slope", [P, PACK], F32)
         neg = sbuf("neg", [P, PACK], F32)
         shift = sbuf("shift", [P, PACK], F32)
+        qrows_il = [sbuf("qrows_il%d" % h, [P, D // 2, PACK], BF16) for h in range(2)]
+        nc.gpsimd.tensor_scalar(qrows_il[0][:], qrows_raw[:, :, 0 : D // 2].rearrange("p t d -> p d t"),
+                                1.0, 0.0, ALU.mult, ALU.add)
+        nc.scalar.copy(qrows_il[1][:].rearrange("p (c i) t -> p c t i", i=4),
+                       qrows_raw[:, :, D // 2 :].rearrange("p t (c i) -> p c t i", i=4))
+
+        dp = sbuf("dp", [P, PACK, I], F32)
+
+        def shifted(r0):
+            nc.vector.tensor_tensor(shift[:, r0 : r0 + 2], sum_cp[:, r0 : r0 + 2], neg[:, r0 : r0 + 2], ALU.mult)
+
+        def affine(r):
+            nc.vector.tensor_scalar(dp[:, r, :], cs[:, r, :], slope[:, r : r + 1], shift[:, r : r + 1],
+                                    ALU.mult, ALU.add)
+
         weigh(0)
         nc.vector.tensor_tensor(z[:], sum_part[:], base[:], ALU.add)
         weigh(1)
         nc.vector.reciprocal(inv_z[:], z[:])
         weigh(2)
         nc.vector.tensor_tensor(slope[:], qs_t[:], inv_z[:], ALU.mult)
-        weigh(3)
+        qrows_first = quantize("qrows_first", qrows_il[0][:, 0:P, :].rearrange("p d t -> p (d t)"), P)
         nc.vector.scalar_tensor_tensor(neg[:], inv_z[:], -1.0, slope[:], ALU.mult, ALU.mult)
-        nc.vector.tensor_tensor(shift[:], sum_cp[:], neg[:], ALU.mult)
-
-        turned_fade = bank("X0", [P, P])
-        nc.tensor.transpose(turned_fade[:], fade_rows[:], ident[:])
-        cols_t = sbuf("cols_t", [P, 8], F32)
-        nc.scalar.copy(cols_t[:], turned_fade[:, 0:8])
-
-        qrows_il = sbuf("qrows_il", [P, D, PACK], BF16)
-        nc.gpsimd.tensor_scalar(qrows_il[:, 0 : D // 2, :], qrows_raw[:, :, 0 : D // 2].rearrange("p t d -> p d t"),
-                                1.0, 0.0, ALU.mult, ALU.add)
-        nc.scalar.copy(qrows_il[:, D // 2 :, :].rearrange("p (c i) t -> p c t i", i=4),
-                       qrows_raw[:, :, D // 2 :].rearrange("p t (c i) -> p c t i", i=4))
-
-        dp = sbuf("dp", [P, PACK, I], F32)
+        weigh(3)
+        shifted(0)
+        shifted(2)
         for r in range(PACK):
-            nc.vector.tensor_scalar(dp[:, r, :], cs[:, r, :], slope[:, r : r + 1], shift[:, r : r + 1],
-                                    ALU.mult, ALU.add)
-        qrows_q = quantize("qrows", qrows_il[:].rearrange("p d t -> p (d t)"), D)
+            affine(r)
         gs = sbuf("gs", [P, I, PACK], BF16)
         nc.vector.tensor_tensor(gs[:].rearrange("p (c i) r -> p c r i", i=4),
                                 dp[:].rearrange("p r (c i) -> p c r i", i=4),
                                 sig[:].rearrange("p r (c i) -> p c r i", i=4), ALU.mult)
         gs_q = quantize("gs", gs[:].rearrange("p i r -> p (i r)"), I)
+        rest_codes = sbuf("rest_codes", [P, 3 * P], U32, tag="dp")
+        rest_plane = sbuf("rest_plane", [P, 3 * P], U8)
+        qrows_rest = (rest_codes, rest_plane)
+        nc.vector.quantize_mx(out=rest_codes[:, 0:P].bitcast(FP8X4), scales=rest_plane[:, 0:P],
+                              in_=qrows_il[0][:, P:, :].rearrange("p d t -> p (d t)"))
+        nc.vector.quantize_mx(out=rest_codes[:, P:].bitcast(FP8X4), scales=rest_plane[:, P:],
+                              in_=qrows_il[1][:].rearrange("p d t -> p (d t)"))
 
-        def fade_pair(g, tags):
-            ft = sbuf("faded_t%d" % g, [P, 8, 2, P], F32)
+        def fade_pair(g, tags, tag=None):
+            ft = sbuf("faded_t%d" % g, [P, 8, 2, P], F32, tag=tag)
             for bb in range(4):
                 stage = bank(tags[bb], [P, 2, 2, P])
                 for b2 in range(2):
@@ -241,24 +255,24 @@ def tile_attend_bsoftthreshold_k_kernel(tc, query, keys_words, keys_scales, th, 
             queue.dma_start(out[j * P : (j + 1) * P, h * BANK : (h + 1) * BANK], res[:])
 
         ft0 = fade_pair(0, ("X0", "X1", "C0", "C1"))
+        faded = {}
+        for h in range(2):
+            for j in range(2):
+                faded[j, h] = to_sbuf(j, h, turn_back(ft0, j, h, "AY"[j] + str(h)))
         gk = [sbuf("gk%d" % j, [P, I], F32) for j in range(4)]
         first = bank("C1", [P, I])
-        product(0, first[:], qrows_q, gs_q)
+        product(0, first[:], qrows_first, gs_q)
         nc.vector.tensor_copy(gk[0][:], first[:])
-        faded = {}
-        for j in range(2):
-            for h in range(2):
-                faded[j, h] = to_sbuf(j, h, turn_back(ft0, j, h, "AY"[j] + str(h)))
         middle = bank("C0", [P, 2, I])
         for j in (1, 2):
-            product(j, middle[:, j - 1, :], qrows_q, gs_q)
+            product(j - 1, middle[:, j - 1, :], qrows_rest, gs_q)
         for j in (1, 2):
             nc.scalar.copy(gk[j][:], middle[:, j - 1, :])
         last = bank("C1", [P, I])
-        product(3, last[:], qrows_q, gs_q)
+        product(2, last[:], qrows_rest, gs_q)
         nc.scalar.copy(gk[3][:], last[:])
 
-        ft1 = fade_pair(1, ("X0", "X1", "X0", "X1"))
+        ft1 = fade_pair(1, ("X0", "X1", "C0", "C1"), tag="dp")
         faded[2, 0] = to_sbuf(2, 0, turn_back(ft1, 2, 0, "A0"))
         faded[2, 1] = turn_back(ft1, 2, 1, "A1")
         for h in range(2):

@@ -102,8 +102,8 @@ def tile_attend_bsoftthreshold_k_kernel(tc, query, keys_words, keys_scales, th, 
             engine_copy(dealt[:, :, 64 * h + s0 : 64 * h + s1, :].rearrange("p r s j -> p s j r"),
                         raw[h][:].rearrange("p j (s r) -> p s j r", r=PACK)[:, s0:s1])
 
-        def quantize(name, src, width):
-            codes = sbuf(name + "_codes", [P, width], U32)
+        def quantize(name, src, width, tag=None):
+            codes = sbuf(name + "_codes", [P, width], U32, tag=tag)
             plane = sbuf(name + "_scales", [P, width], U8)
             nc.vector.quantize_mx(out=codes[:].bitcast(FP8X4), scales=plane[:], in_=src)
             return codes, plane
@@ -123,11 +123,12 @@ def tile_attend_bsoftthreshold_k_kernel(tc, query, keys_words, keys_scales, th, 
         deal(nc.scalar.copy, query_dealt, query_raw, 0, 0, 64)
         deal(nc.scalar.copy, query_dealt, query_raw, 1, 0, 20)
         deal(nc.vector.tensor_copy, query_dealt, query_raw, 1, 20, 64)
-        query_q = quantize("query", query_dealt[:].rearrange("p r s j -> p (r s j)"), Q)
+        query_q = [quantize("query0", query_dealt[:, 0:2].rearrange("p r s j -> p (r s j)"), 2 * P)]
         key_words_g = gather("key_words_g", key_words, U32)
+        query_q.append(quantize("query1", query_dealt[:, 2:4].rearrange("p r s j -> p (r s j)"), 2 * P, tag="key_words"))
         scores = [bank(tag, [P, I]) for tag in ("A0", "A1", "Y0", "Y1")]
         for r in range(PACK):
-            product(r, scores[r][:], query_q, (key_words_g, key_plane_g))
+            product(r % 2, scores[r][:], query_q[r // 2], (key_words_g, key_plane_g))
 
         neg_th = sbuf("neg_th", [P, PACK], F32)
         nc.gpsimd.tensor_scalar(neg_th[:], th_t[:], -1.0, 0.0, ALU.mult, ALU.add)
@@ -149,8 +150,9 @@ def tile_attend_bsoftthreshold_k_kernel(tc, query, keys_words, keys_scales, th, 
         gout_dealt = sbuf("gout_dealt", [P, PACK, P, PACK], BF16)
         deal(nc.vector.tensor_copy, gout_dealt, gout_raw, 0, 0, 64)
         deal(nc.vector.tensor_copy, gout_dealt, gout_raw, 1, 0, 64)
-        gout_q = quantize("gout", gout_dealt[:].rearrange("p r s j -> p (r s j)"), Q)
+        gout_q = [quantize("gout0", gout_dealt[:, 0:2].rearrange("p r s j -> p (r s j)"), 2 * P)]
         val_words_g = gather("val_words_g", val_words, U32)
+        gout_q.append(quantize("gout1", gout_dealt[:, 2:4].rearrange("p r s j -> p (r s j)"), 2 * P, tag="val_words"))
         turned_fade = bank("X0", [P, P])
         nc.tensor.transpose(turned_fade[:], fade_rows[:], ident[:])
         cols_t = sbuf("cols_t", [P, 8], F32)
@@ -159,7 +161,7 @@ def tile_attend_bsoftthreshold_k_kernel(tc, query, keys_words, keys_scales, th, 
         cs = sbuf("cs", [P, PACK, I], F32)
         for r, tag in enumerate(("C0", "C1", "X0", "X1")):
             c0 = bank(tag, [P, I])
-            product(r, c0[:], gout_q, (val_words_g, val_plane_g))
+            product(r % 2, c0[:], gout_q[r // 2], (val_words_g, val_plane_g))
             nc.vector.tensor_tensor(cs[:, r, :], c0[:], size_t[:], ALU.mult)
 
         part = sbuf("part", [P, PACK, I], F32)
@@ -256,19 +258,20 @@ def tile_attend_bsoftthreshold_k_kernel(tc, query, keys_words, keys_scales, th, 
 
         ft0 = fade_pair(0, ("X0", "X1", "C0", "C1"))
         faded = {}
-        for h in range(2):
-            for j in range(2):
-                faded[j, h] = to_sbuf(j, h, turn_back(ft0, j, h, "AY"[j] + str(h)))
+        for j in range(2):
+            faded[j, 0] = to_sbuf(j, 0, turn_back(ft0, j, 0, "AY"[j] + "0"))
         gk = [sbuf("gk%d" % j, [P, I], F32) for j in range(4)]
-        first = bank("C1", [P, I])
+        first = bank("C0", [P, I])
         product(0, first[:], qrows_first, gs_q)
         nc.vector.tensor_copy(gk[0][:], first[:])
-        middle = bank("C0", [P, 2, I])
+        middle = bank("C1", [P, 2, I])
         for j in (1, 2):
             product(j - 1, middle[:, j - 1, :], qrows_rest, gs_q)
         for j in (1, 2):
             nc.scalar.copy(gk[j][:], middle[:, j - 1, :])
-        last = bank("C1", [P, I])
+        for j in range(2):
+            faded[j, 1] = to_sbuf(j, 1, turn_back(ft0, j, 1, "AY"[j] + "1"))
+        last = bank("C0", [P, I])
         product(2, last[:], qrows_rest, gs_q)
         nc.scalar.copy(gk[3][:], last[:])
 

from contextlib import ExitStack

import concourse.mybir as mybir
from concourse.masks import make_identity

D, E, T, I, Q, U = 512, 512, 1024, 256, 512, 1024
FLOPS = 2 * I * Q * (D + E + D)

F32 = mybir.dt.float32
BF16 = mybir.dt.bfloat16
I32 = mybir.dt.int32
U32 = mybir.dt.uint32
U16 = mybir.dt.uint16
U8 = mybir.dt.uint8
FP8X4 = mybir.dt.float8_e4m3fn_x4
ALU = mybir.AluOpType
ACT = mybir.ActivationFunctionType

P = 128
PACK = 4
BANK = 512


def tile_attend_bsoftthreshold_k_kernel(tc, query, keys_words, keys_scales, th, reserve, gout, vals_words,
                                         vals_scales, size, qs, qrows, old, fade, offs, offs4, out):
    nc = tc.nc
    with ExitStack() as ctx:
        lists = ctx.enter_context(tc.tile_pool(name="lists", bufs=1))
        sb = ctx.enter_context(tc.tile_pool(name="sb", bufs=1))
        ps = ctx.enter_context(tc.psum_pool(name="ps", bufs=1))

        def sbuf(name, shape, dtype, tag=None):
            return sb.tile(shape, dtype, name=name, tag=tag or name, align_bytes=64)

        def bank(tag, shape):
            return ps.tile(shape, F32, name=tag, tag=tag)

        key_plane = sbuf("key_plane", [P, T], U8)
        val_plane = sbuf("val_plane", [P, T], U8)
        half = sbuf("half", [P, 1], F32)
        nc.vector.memset(half[:], 0.5)
        minus_half = sbuf("minus_half", [P, 1], F32)
        nc.vector.memset(minus_half[:], -0.5)
        fade_rows = sbuf("fade_rows", [P, P], F32)
        size_t = sbuf("size_t", [P, I], F32)
        windows = [sbuf("window%d" % j, [P, U], F32) for j in range(4)]
        for j in range(4):
            (nc.vector if j < 2 else nc.gpsimd).memset(windows[j][:], 0.0)
        ident = sbuf("ident", [P, P], F32)
        make_identity(nc, ident[:])

        slots = lists.tile([P, I // 16], U16, name="slots")
        places = lists.tile([P, I // 16], U16, name="places")
        query_raw = [sbuf("query_raw%d" % h, [P, PACK, Q // 2], F32) for h in range(2)]
        gout_raw = [sbuf("gout_raw%d" % h, [P, PACK, Q // 2], F32) for h in range(2)]
        qrows_raw = sbuf("qrows_raw", [P, PACK, D], F32)
        key_words = sbuf("key_words", [P, T], U32)
        val_words = sbuf("val_words", [P, T], U32)
        th_t = sbuf("th_t", [P, PACK], F32)
        reserve_t = sbuf("reserve_t", [P, PACK], F32)
        qs_t = sbuf("qs_t", [P, PACK], F32)
        old_t = [sbuf("old%d" % g, [P, 2, U], F32) for g in range(2)]

        def load_plane(queue, plane, scales, quads):
            for quad in quads:
                queue.dma_start(plane[32 * quad : 32 * quad + 32, :].bitcast(I32),
                                scales[0, 4 * quad : 4 * quad + 4, :].bitcast(I32).partition_broadcast(8))

        def load_words(words, src):
            nc.sync.dma_start(words[:].bitcast(I32), src[0].rearrange("p n t -> p (n t)").bitcast(I32))

        def by_row(vec):
            return vec.rearrange("(p r) o -> p (r o)", r=PACK)

        def load_half(raw, src, h):
            cols = slice(h * (Q // 2), (h + 1) * (Q // 2))
            nc.sync.dma_start(raw[h][:], src[:, cols].rearrange("(p j) q -> p j q", j=PACK))

        load_half(query_raw, query, 0)
        nc.sync.dma_start(slots[:], offs)
        load_plane(nc.sync, key_plane, keys_scales, range(4))
        load_half(query_raw, query, 1)
        load_words(key_words, keys_words)
        nc.sync.dma_start(th_t[:], by_row(th))
        load_plane(nc.sync, val_plane, vals_scales, range(4))
        load_half(gout_raw, gout, 0)
        load_half(gout_raw, gout, 1)
        load_words(val_words, vals_words)
        nc.sync.dma_start(fade_rows[:], fade.rearrange("o (b x) -> (o b) x", x=P).partition_broadcast(16))
        nc.sync.dma_start(size_t[:], size[0].partition_broadcast(P))
        nc.sync.dma_start(reserve_t[:], by_row(reserve))
        nc.sync.dma_start(qs_t[:], by_row(qs))
        nc.sync.dma_start(qrows_raw[:], qrows.rearrange("(p j) d -> p j d", j=PACK))
        for g in range(2):
            nc.sync.dma_start(old_t[g][:], old[2 * P * g : 2 * P * (g + 1), :].rearrange("(j p) u -> p j u", p=P))
        nc.sync.dma_start(places[:], offs4)

        warm = sbuf("warm", [P, 1], F32)
        nc.scalar.activation(warm[:], half[:], ACT.Sigmoid)

        def deal(engine_copy, dealt, raw, h, s0, s1):
            engine_copy(dealt[:, :, 64 * h + s0 : 64 * h + s1, :].rearrange("p r s j -> p s j r"),
                        raw[h][:].rearrange("p j (s r) -> p s j r", r=PACK)[:, s0:s1])

        def quantize(name, src, width, tag=None):
            codes = sbuf(name + "_codes", [P, width], U32, tag=tag)
            plane = sbuf(name + "_scales", [P, width], U8)
            nc.vector.quantize_mx(out=codes[:].bitcast(FP8X4), scales=plane[:], in_=src)
            return codes, plane

        def gather(name, window, dtype):
            picked = sbuf(name, [P, I], dtype)
            nc.vector.tensor_copy(picked[:], window[:].indirect(slots[:]))
            return picked

        def product(m, dst, stationary, moving):
            cols = slice(m * P, (m + 1) * P)
            nc.tensor.matmul_mx(out=dst, lhsT=stationary[0][:, cols].bitcast(FP8X4), lhsT_scale=stationary[1][:, cols],
                                rhs=moving[0][:].bitcast(FP8X4), rhs_scale=moving[1][:], start=True, stop=True)

        key_plane_g = gather("key_plane_g", key_plane, U8)
        query_dealt = sbuf("query_dealt", [P, PACK, P, PACK], BF16)
        deal(nc.scalar.copy, query_dealt, query_raw, 0, 0, 64)
        deal(nc.scalar.copy, query_dealt, query_raw, 1, 0, 20)
        deal(nc.vector.tensor_copy, query_dealt, query_raw, 1, 20, 64)
        query_q = [quantize("query0", query_dealt[:, 0:2].rearrange("p r s j -> p (r s j)"), 2 * P)]
        key_words_g = gather("key_words_g", key_words, U32)
        query_q.append(quantize("query1", query_dealt[:, 2:4].rearrange("p r s j -> p (r s j)"), 2 * P, tag="key_words"))
        scores = [bank(tag, [P, I]) for tag in ("A0", "A1", "Y0", "Y1")]
        for r in range(PACK):
            product(r % 2, scores[r][:], query_q[r // 2], (key_words_g, key_plane_g))

        neg_th = sbuf("neg_th", [P, PACK], F32)
        nc.gpsimd.tensor_scalar(neg_th[:], th_t[:], -1.0, 0.0, ALU.mult, ALU.add)
        th_sum = sbuf("th_sum", [P, PACK], F32)
        nc.gpsimd.tensor_scalar(th_sum[:], th_t[:], -float(I), 0.0, ALU.mult, ALU.add)
        base = sbuf("base", [P, PACK], F32)
        nc.gpsimd.tensor_tensor(base[:], th_sum[:], reserve_t[:], ALU.add)

        sig = sbuf("sig", [P, PACK, I], F32)
        for r in range(PACK):
            nc.scalar.activation(sig[:, r, :], scores[r][:], ACT.Sigmoid, bias=neg_th[:, r : r + 1])
        dist = sbuf("dist", [P, PACK * I], F32)
        nc.scalar.activation(dist[:], sig[:].rearrange("p r i -> p (r i)"), ACT.Abs, bias=minus_half[:])
        logm = sbuf("logm", [P, PACK, I], F32)
        for r in range(PACK):
            nc.scalar.activation(logm[:, r, :], dist[:, r * I : (r + 1) * I], ACT.Ln, bias=half[:])

        val_plane_g = gather("val_plane_g", val_plane, U8)
        gout_dealt = sbuf("gout_dealt", [P, PACK, P, PACK], BF16)
        deal(nc.vector.tensor_copy, gout_dealt, gout_raw, 0, 0, 64)
        deal(nc.vector.tensor_copy, gout_dealt, gout_raw, 1, 0, 64)
        gout_q = [quantize("gout0", gout_dealt[:, 0:2].rearrange("p r s j -> p (r s j)"), 2 * P)]
        val_words_g = gather("val_words_g", val_words, U32)
        gout_q.append(quantize("gout1", gout_dealt[:, 2:4].rearrange("p r s j -> p (r s j)"), 2 * P, tag="val_words"))
        turned_fade = bank("X0", [P, P])
        nc.tensor.transpose(turned_fade[:], fade_rows[:], ident[:])
        cols_t = sbuf("cols_t", [P, 8], F32)
        nc.vector.tensor_copy(cols_t[:], turned_fade[:, 0:8])

        cs = sbuf("cs", [P, PACK, I], F32)
        for r, tag in enumerate(("C0", "C1", "X0", "X1")):
            c0 = bank(tag, [P, I])
            product(r % 2, c0[:], gout_q[r // 2], (val_words_g, val_plane_g))
            nc.vector.tensor_tensor(cs[:, r, :], c0[:], size_t[:], ALU.mult)

        part = sbuf("part", [P, PACK, I], F32)
        sum_part = sbuf("sum_part", [P, PACK], F32)
        for r in range(PACK):
            nc.vector.scalar_tensor_tensor(part[:, r, :], scores[r][:], th_t[:, r : r + 1],
                                           logm[:, r, :], ALU.max, ALU.subtract, accum_out=sum_part[:, r : r + 1])
        weighted = sbuf("weighted", [P, PACK, I], F32)
        sum_cp = sbuf("sum_cp", [P, PACK], F32)

        def weigh(r):
            nc.vector.scalar_tensor_tensor(weighted[:, r, :], part[:, r, :], th_t[:, r : r + 1], cs[:, r, :],
                                           ALU.subtract, ALU.mult, accum_out=sum_cp[:, r : r + 1])

        z = sbuf("z", [P, PACK], F32)
        inv_z = sbuf("inv_z", [P, PACK], F32)
        slope = sbuf("slope", [P, PACK], F32)
        neg = sbuf("neg", [P, PACK], F32)
        shift = sbuf("shift", [P, PACK], F32)
        qrows_il = [sbuf("qrows_il%d" % h, [P, D // 2, PACK], BF16) for h in range(2)]
        nc.gpsimd.tensor_scalar(qrows_il[0][:], qrows_raw[:, :, 0 : D // 2].rearrange("p t d -> p d t"),
                                1.0, 0.0, ALU.mult, ALU.add)
        nc.scalar.copy(qrows_il[1][:].rearrange("p (c i) t -> p c t i", i=4),
                       qrows_raw[:, :, D // 2 :].rearrange("p t (c i) -> p c t i", i=4))

        dp = sbuf("dp", [P, PACK, I], F32)

        def shifted(r0):
            nc.vector.tensor_tensor(shift[:, r0 : r0 + 2], sum_cp[:, r0 : r0 + 2], neg[:, r0 : r0 + 2], ALU.mult)

        def affine(r):
            nc.vector.tensor_scalar(dp[:, r, :], cs[:, r, :], slope[:, r : r + 1], shift[:, r : r + 1],
                                    ALU.mult, ALU.add)

        weigh(0)
        nc.vector.tensor_tensor(z[:], sum_part[:], base[:], ALU.add)
        weigh(1)
        nc.vector.reciprocal(inv_z[:], z[:])
        weigh(2)
        nc.vector.tensor_tensor(slope[:], qs_t[:], inv_z[:], ALU.mult)
        qrows_first = quantize("qrows_first", qrows_il[0][:, 0:P, :].rearrange("p d t -> p (d t)"), P)
        nc.vector.scalar_tensor_tensor(neg[:], inv_z[:], -1.0, slope[:], ALU.mult, ALU.mult)
        weigh(3)
        shifted(0)
        shifted(2)
        for r in range(PACK):
            affine(r)
        gs = sbuf("gs", [P, I, PACK], BF16)
        nc.vector.tensor_tensor(gs[:].rearrange("p (c i) r -> p c r i", i=4),
                                dp[:].rearrange("p r (c i) -> p c r i", i=4),
                                sig[:].rearrange("p r (c i) -> p c r i", i=4), ALU.mult)
        gs_q = quantize("gs", gs[:].rearrange("p i r -> p (i r)"), I)
        rest_codes = sbuf("rest_codes", [P, 3 * P], U32, tag="dp")
        rest_plane = sbuf("rest_plane", [P, 3 * P], U8)
        qrows_rest = (rest_codes, rest_plane)
        nc.vector.quantize_mx(out=rest_codes[:, 0:P].bitcast(FP8X4), scales=rest_plane[:, 0:P],
                              in_=qrows_il[0][:, P:, :].rearrange("p d t -> p (d t)"))
        nc.vector.quantize_mx(out=rest_codes[:, P:].bitcast(FP8X4), scales=rest_plane[:, P:],
                              in_=qrows_il[1][:].rearrange("p d t -> p (d t)"))

        def fade_pair(g, tags, tag=None):
            ft = sbuf("faded_t%d" % g, [P, 8, 2, P], F32, tag=tag)
            for bb in range(4):
                stage = bank(tags[bb], [P, 2, 2, P])
                for b2 in range(2):
                    b = 2 * bb + b2
                    for jj in range(2):
                        nc.tensor.transpose(stage[:, b2, jj, :], old_t[g][:, jj, b * P : (b + 1) * P], ident[:])
                for b2 in range(2):
                    b = 2 * bb + b2
                    nc.scalar.activation(ft[:, b].rearrange("p j d -> p (j d)"),
                                         stage[:, b2].rearrange("p j d -> p (j d)"), ACT.Copy,
                                         scale=cols_t[:, b : b + 1])
            return ft

        def turn_back(ft, j, h, tag):
            faded = bank(tag, [P, 4, P])
            for b in range(4):
                nc.tensor.transpose(faded[:, b, :], ft[:, 4 * h + b, j % 2, :], ident[:])
            return faded[:].rearrange("p b d -> p (b d)")

        def to_sbuf(j, h, faded):
            held = sbuf("held%d_%d" % (j, h), [P, BANK], F32)
            nc.scalar.copy(held[:], faded)
            return held[:]

        def scatter(j):
            nc.vector.tensor_copy(windows[j][:].indirect(places[:]), gk[j][:])

        def finish(engine, queue, j, h, faded):
            res = sbuf("res%d_%d" % (j, h), [P, BANK], F32)
            engine.tensor_tensor(res[:], faded, windows[j][:, h * BANK : (h + 1) * BANK], ALU.add)
            queue.dma_start(out[j * P : (j + 1) * P, h * BANK : (h + 1) * BANK], res[:])

        ft0 = fade_pair(0, ("X0", "X1", "C0", "C1"))
        faded = {}
        for j in range(2):
            faded[j, 0] = to_sbuf(j, 0, turn_back(ft0, j, 0, "AY"[j] + "0"))
        gk = [sbuf("gk%d" % j, [P, I], F32) for j in range(4)]
        first = bank("C0", [P, I])
        product(0, first[:], qrows_first, gs_q)
        nc.vector.tensor_copy(gk[0][:], first[:])
        middle = bank("C1", [P, 2, I])
        for j in (1, 2):
            product(j - 1, middle[:, j - 1, :], qrows_rest, gs_q)
        for j in (1, 2):
            nc.scalar.copy(gk[j][:], middle[:, j - 1, :])
        for j in range(2):
            faded[j, 1] = to_sbuf(j, 1, turn_back(ft0, j, 1, "AY"[j] + "1"))
        last = bank("C0", [P, I])
        product(2, last[:], qrows_rest, gs_q)
        nc.scalar.copy(gk[3][:], last[:])

        ft1 = fade_pair(1, ("X0", "X1", "C0", "C1"), tag="dp")
        faded[2, 0] = to_sbuf(2, 0, turn_back(ft1, 2, 0, "A0"))
        faded[2, 1] = turn_back(ft1, 2, 1, "A1")
        for h in range(2):
            faded[3, h] = turn_back(ft1, 3, h, "Y%d" % h)

        for j in range(3):
            scatter(j)
        for j, h in ((0, 0), (0, 1), (1, 0), (1, 1), (2, 0)):
            finish(nc.gpsimd, nc.sync, j, h, faded[j, h])
        finish(nc.vector, nc.scalar, 2, 1, faded[2, 1])
        scatter(3)
        for h in range(2):
            finish(nc.vector, nc.scalar, 3, h, faded[3, h])
